import numpy as np
import ml_dtypes


def mxq(x, axis, fmt="e4m3"):
    dtype, down = {"e4m3": (ml_dtypes.float8_e4m3fn, 7), "e5m2": (ml_dtypes.float8_e5m2, 14)}[fmt]
    v = np.moveaxis(np.asarray(x, np.float32).astype(ml_dtypes.bfloat16).astype(np.float64), axis, -1)
    blocks = v.reshape(v.shape[:-1] + (-1, 32))
    amax = np.abs(blocks).max(-1, keepdims=True)
    byte = np.maximum(np.where(amax > 0, np.frexp(amax)[1] - 1 + 127, 0) - down, 1)
    scale = np.exp2(byte - 127.0)
    codes = (blocks / scale).astype(np.float32).astype(dtype).astype(np.float64)
    return np.moveaxis((codes * scale).reshape(v.shape), -1, axis)


WIDE = False


def mx_kscale(k):
    if not WIDE:
        return np.ones(k)
    levels = np.array([10, -10, 5, -5, 0])
    if k % 512:
        return np.exp2(np.random.permutation(np.resize(levels, k // 32))).repeat(32)
    a = np.empty((k // 512, 16))
    for p in range(k // 512):
        a[p, :8] = np.random.permutation(np.resize(levels, 8))
        for g in range(8):
            far = levels[np.abs(levels - a[p, g]) >= 10]
            a[p, g + 8] = far[np.random.randint(len(far))]
    return np.exp2(a.ravel()).repeat(32)


BF16 = ml_dtypes.bfloat16


def bf(x):
    return np.asarray(x, np.float32).astype(BF16)


def f64(x):
    return np.asarray(x).astype(np.float64)


E2M1 = np.array([0.0, 0.5, 1.0, 1.5, 2.0, 3.0, 4.0, 6.0, -0.0, -0.5, -1.0, -1.5, -2.0, -3.0, -4.0, -6.0])


def pack_weight(w, fmt):
    k, n = w.shape
    w = f64(bf(w)).reshape(k // 32, 32, n)
    amax = np.abs(w).max(1)
    if fmt == "e4m3":
        byte = np.frexp(amax)[1] - 1 + 127 - 7
    else:
        mant, ex = np.frexp(amax / 6.0)
        byte = np.where(mant > 0.5, ex, ex - 1) + 127
    byte = np.clip(np.where(amax > 0, byte, 1), 1, 254)
    scaled = (w * np.exp2(127.0 - byte)[:, None, :]).reshape(k, n).astype(np.float32)
    by_word = np.ascontiguousarray(scaled.reshape(k // 512, 128, 4, n).transpose(0, 1, 3, 2))
    if fmt == "e4m3":
        words = by_word.astype(ml_dtypes.float8_e4m3fn).view(np.uint8)
    else:
        c = by_word.astype(ml_dtypes.float4_e2m1fn).view(np.uint8) & 0xF
        words = c[..., 0::2] | (c[..., 1::2] << 4)
    return np.ascontiguousarray(words), np.ascontiguousarray(byte.astype(np.uint8).reshape(k // 512, 16, n))


def unpack_weight(words, scales, fmt):
    g, p, n, _ = words.shape
    if fmt == "e4m3":
        vals = np.ascontiguousarray(words).view(ml_dtypes.float8_e4m3fn).astype(np.float64)
    else:
        nib = np.empty((g, p, n, 4), np.uint8)
        nib[..., 0::2] = words & 0xF
        nib[..., 1::2] = words >> 4
        vals = E2M1[nib]
    vals = vals * np.repeat(np.exp2(scales.astype(np.float64) - 127.0), 8, axis=1)[..., None]
    return vals.transpose(0, 1, 3, 2).reshape(g * 512, n)
def pack4(w):
    words, scales = pack_weight(w, "e2m1")
    return words.reshape(words.shape[0], 128, -1), scales


def unpack4(words, scales):
    return unpack_weight(words.reshape(words.shape[0], 128, -1, 2), scales, "e2m1")


G, T, K, F, V = 2, 512, 1024, 1024, 3072


def setup_inputs():
    s = mx_kscale(G * K).reshape(G, K)
    t = mx_kscale(G * F).reshape(G, F)
    x = np.random.standard_normal((G, T, K)) * s[:, None, :]
    w1 = np.random.standard_normal((G, K, F)) / np.sqrt(K) / s[:, :, None] * t[:, None, :]
    w2 = np.random.standard_normal((G, F, V)) / np.sqrt(F) / t[:, :, None]
    w1_words, w1_scales = pack4(w1.reshape(G * K, F))
    w2_words, w2_scales = pack4(w2.reshape(G * F, V))
    alpha = np.random.uniform(0.2, 0.8, T)
    return {"x": bf(x),
            "w1_words": w1_words, "w1_scales": w1_scales,
            "w2_words": w2_words, "w2_scales": w2_scales,
            "alpha": bf(alpha)}


def reference(x, w1_words, w1_scales, w2_words, w2_scales, alpha):
    x, alpha = f64(x), f64(alpha)
    w1 = unpack4(w1_words, w1_scales).reshape(G, K, F)
    w2 = unpack4(w2_words, w2_scales).reshape(G, F, V)
    z = []
    for m in range(G):
        h = mxq(x[m], 1, "e4m3") @ w1[m]
        h = np.maximum(h, 0.0)
        z.append(mxq(h, 1, "e4m3") @ w2[m])
    return z[0] - alpha[:, None] * z[1]

@@ -1,0 +1,344 @@
+from contextlib import ExitStack
+
+import concourse.mybir as mybir
+from concourse.masks import make_identity
+
+F32 = mybir.dt.float32
+BF16 = mybir.dt.bfloat16
+U32 = mybir.dt.uint32
+I32 = mybir.dt.int32
+U8 = mybir.dt.uint8
+FP8X4 = mybir.dt.float8_e4m3fn_x4
+FP4X4 = mybir.dt.float4_e2m1fn_x4
+RELU = mybir.ActivationFunctionType.Relu
+COPY = mybir.ActivationFunctionType.Copy
+MULT = mybir.AluOpType.mult
+ADD = mybir.AluOpType.add
+
+T, K, F, V = 512, 1024, 1024, 3072
+P = 128
+FLOPS = 2 * 2 * T * K * F + 2 * 2 * T * F * V
+
+
+def tile_contrastive_decoding_logits_s14_kernel(tc, x, w1_words, w1_scales, w2_words, w2_scales, alpha, out):
+    nc = tc.nc
+    with ExitStack() as ctx:
+        keep = ctx.enter_context(tc.tile_pool(name="keep", bufs=1))
+        zpool = ctx.enter_context(tc.tile_pool(name="zpool", bufs=14))
+        opool = ctx.enter_context(tc.tile_pool(name="opool", bufs=6))
+        psum = ctx.enter_context(tc.psum_pool(name="psum", bufs=8))
+        ctx.enter_context(tc.manual_schedule())
+
+        def bank():
+            b = psum.tile([P, 512], F32, name="bank")
+            return b
+
+        def sb(name, shape, dt):
+            t = keep.tile(shape, dt, name=name, align_bytes=256)
+            return t
+
+        xs = [[sb("x%d_%d" % (m, i), [P, K], BF16) for i in range(4)] for m in range(2)]
+        xg0 = [sb("xg0_%d" % i, [P, 2, P, 4], BF16) for i in range(4)]
+        xq0 = [sb("xq0_%d" % i, [P, 2, P], U32) for i in range(4)]
+        xqs0 = [sb("xqs0_%d" % i, [P, 2, P], U8) for i in range(4)]
+        xg1 = sb("xg1", [P, 2, T, 4], BF16)
+        xq1 = [sb("xq1_%d" % g, [P, T], U32) for g in range(2)]
+        xqs1 = [sb("xqs1_%d" % g, [P, T], U8) for g in range(2)]
+        w1r = [sb("w1r%d" % m, [P, 2, 2, 1024], U8) for m in range(2)]
+        w1p = [sb("w1p%d" % m, [P, 2, 2, 4, 256], U8) for m in range(2)]
+        w1sr = [sb("w1sr%d" % m, [P, 2, 1024], U8) for m in range(2)]
+        w1sp = [sb("w1sp%d" % m, [P, 2, 2, 512], U8) for m in range(2)]
+        w2t = [[sb("w2_%d_%d" % (m, vp), [P, 2, 2048], U8) for vp in range(3)] for m in range(2)]
+        w2s = sb("w2s", [P, 4, V], U8)
+        hb0 = [sb("hb0_%d" % i, [P, 2, P, 4], BF16) for i in range(4)]
+        hq0 = [sb("hq0_%d" % i, [P, 2, P], U32) for i in range(4)]
+        hqs0 = [sb("hqs0_%d" % i, [P, 2, P], U8) for i in range(4)]
+        hr1 = [sb("hr1_%d" % g, [P, 4, T], BF16) for g in range(2)]
+        hb1 = [sb("hb1_%d" % g, [P, T, 4], BF16) for g in range(2)]
+        hq1 = [sb("hq1_%d" % g, [P, T], U32) for g in range(2)]
+        hqs1 = [sb("hqs1_%d" % g, [P, T], U8) for g in range(2)]
+        ident = sb("ident", [P, P], F32)
+        abf = sb("abf", [P, P], BF16)
+        af = sb("af", [P, P], F32)
+        nega = sb("nega", [P, 4], F32)
+        warm = sb("warm", [P, 2], F32)
+
+        def load_x(m, i):
+            nc.sync.dma_start(out=xs[m][i][:], in_=x[m, P * i : P * (i + 1), :])
+
+        def load_w1(m, G):
+            nc.sync.dma_start(
+                out=w1r[m][:, G, :, :].bitcast(I32),
+                in_=w1_words[2 * m : 2 * m + 2, :, 1024 * G : 1024 * (G + 1)].rearrange("g p c -> p g c").bitcast(I32),
+            )
+
+        def load_w1s(m):
+            src = w1_scales[2 * m : 2 * m + 2].rearrange("g (q r) n -> r q g n", r=4)
+            for r in range(4):
+                nc.sync.dma_start(out=w1sr[m][r:P:32, :, :].bitcast(I32), in_=src[r].bitcast(I32))
+
+        def load_w2(m, vp):
+            nc.sync.dma_start(
+                out=w2t[m][vp][:].bitcast(I32),
+                in_=w2_words[2 * m : 2 * m + 2, :, 2048 * vp : 2048 * (vp + 1)].rearrange("g p c -> p g c").bitcast(I32),
+            )
+
+        def load_w2s(lo, hi):
+            src = w2_scales.rearrange("g (q r) n -> r q g n", r=4)
+            for r in range(4):
+                nc.sync.dma_start(out=w2s[r:P:32, :, lo:hi].bitcast(I32), in_=src[r][:, :, lo:hi].bitcast(I32))
+
+        def tx(m, i):
+            b = bank()
+            bv = b[:].rearrange("p (g u r) -> p g u r", g=2, u=2)
+            words = xs[m][i][:].bitcast(F32)
+            for g in range(2):
+                for u in range(2):
+                    nc.tensor.transpose(bv[:, g, u, :], words[:, 256 * g + u : 256 * (g + 1) : 2], ident[:])
+            return bv
+
+        def cx(m, i, bv):
+            src = bv.rearrange("p g u r -> p g r u")
+            if m == 0:
+                dst = xg0[i][:].rearrange("p g r f -> p (g r f)").bitcast(F32).rearrange("p (g r u) -> p g r u", g=2, u=2)
+            else:
+                dst = xg1[:].rearrange("p g r f -> p (g r f)").bitcast(F32).rearrange("p (g r u) -> p g r u", g=2, u=2)[:, :, P * i : P * (i + 1), :]
+            nc.scalar.copy(out=dst, in_=src)
+
+        def qx0(i):
+            nc.vector.quantize_mx(
+                out=xq0[i][:].rearrange("p g r -> p (g r)").bitcast(FP8X4),
+                scales=xqs0[i][:].rearrange("p g r -> p (g r)"),
+                in_=xg0[i][:].rearrange("p g r f -> p (g r f)"),
+            )
+
+        def qx1(g):
+            nc.vector.quantize_mx(
+                out=xq1[g][:].bitcast(FP8X4),
+                scales=xqs1[g][:],
+                in_=xg1[:, g, :, :].rearrange("p r f -> p (r f)"),
+            )
+
+        def perm_codes(m, G, g):
+            nc.vector.tensor_copy(
+                out=w1p[m][:, G, g, :, :].rearrange("p t (m e) -> p t m e", e=2),
+                in_=w1r[m][:, G, g, :].rearrange("p (m t e) -> p t m e", t=4, e=2),
+            )
+
+        def perm_scales(m, G):
+            nc.vector.tensor_copy(
+                out=w1sp[m][:, G, :, :].rearrange("p g (t m) -> p g t m", t=4),
+                in_=w1sr[m][:, :, 512 * G : 512 * (G + 1)].rearrange("p g (m t) -> p g t m", t=4),
+            )
+
+        def s1a(i, G):
+            b = bank()
+            bv = b[:].rearrange("p (t r) -> p t r", t=4)
+            for t in range(4):
+                for g in range(2):
+                    nc.tensor.matmul_mx(
+                        out=bv[:, t, :],
+                        lhsT=w1p[0][:, G, g, t, :].bitcast(FP4X4),
+                        lhsT_scale=w1sp[0][:, G, g, P * t : P * (t + 1)],
+                        rhs=xq0[i][:, g, :].bitcast(FP8X4),
+                        rhs_scale=xqs0[i][:, g, :],
+                        start=(g == 0),
+                        stop=(g == 1),
+                    )
+            return bv
+
+        def r1a(i, G, bv):
+            nc.scalar.activation(out=hb0[i][:, G, :, :], in_=bv.rearrange("p t r -> p r t"), func=RELU)
+
+        def qh0(i):
+            nc.vector.quantize_mx(
+                out=hq0[i][:].rearrange("p g r -> p (g r)").bitcast(FP8X4),
+                scales=hqs0[i][:].rearrange("p g r -> p (g r)"),
+                in_=hb0[i][:].rearrange("p g r f -> p (g r f)"),
+            )
+
+        def s1b(G, t):
+            b = bank()
+            for g in range(2):
+                nc.tensor.matmul_mx(
+                    out=b[:],
+                    lhsT=w1p[1][:, G, g, t, :].bitcast(FP4X4),
+                    lhsT_scale=w1sp[1][:, G, g, P * t : P * (t + 1)],
+                    rhs=xq1[g][:].bitcast(FP8X4),
+                    rhs_scale=xqs1[g][:],
+                    start=(g == 0),
+                    stop=(g == 1),
+                )
+            return b
+
+        def r1b(G, t, b, eng):
+            if eng == "s":
+                nc.scalar.activation(out=hr1[G][:, t, :], in_=b[:], func=RELU)
+            else:
+                nc.vector.tensor_scalar_max(out=hr1[G][:, t, :], in0=b[:], scalar1=0.0)
+
+        def il(G):
+            nc.vector.tensor_copy(out=hb1[G][:], in_=hr1[G][:].rearrange("p t r -> p r t"))
+
+        def qh1(G):
+            nc.vector.quantize_mx(
+                out=hq1[G][:].bitcast(FP8X4),
+                scales=hqs1[G][:],
+                in_=hb1[G][:].rearrange("p r f -> p (r f)"),
+            )
+
+        zs = {}
+
+        def w2_args(m, v, G):
+            lo = 1024 * (v % 2)
+            return (
+                w2t[m][v // 2][:, G, lo : lo + 1024].bitcast(FP4X4),
+                w2s[:, 2 * m + G, 512 * v : 512 * (v + 1)],
+            )
+
+        def z0(v, i):
+            b = bank()
+            for G in range(2):
+                rhs, rhs_scale = w2_args(0, v, G)
+                nc.tensor.matmul_mx(
+                    out=b[:],
+                    lhsT=hq0[i][:, G, :].bitcast(FP8X4),
+                    lhsT_scale=hqs0[i][:, G, :],
+                    rhs=rhs,
+                    rhs_scale=rhs_scale,
+                    start=(G == 0),
+                    stop=(G == 1),
+                )
+            z = zpool.tile([P, 512], F32, name="z")
+            nc.scalar.copy(out=z[:], in_=b[:])
+            zs[(v, i)] = z
+
+        def z1(v, i):
+            b = bank()
+            for G in range(2):
+                rhs, rhs_scale = w2_args(1, v, G)
+                nc.tensor.matmul_mx(
+                    out=b[:],
+                    lhsT=hq1[G][:, P * i : P * (i + 1)].bitcast(FP8X4),
+                    lhsT_scale=hqs1[G][:, P * i : P * (i + 1)],
+                    rhs=rhs,
+                    rhs_scale=rhs_scale,
+                    start=(G == 0),
+                    stop=(G == 1),
+                )
+            o = opool.tile([P, 512], F32, name="o")
+            nc.vector.scalar_tensor_tensor(
+                out=o[:], in0=b[:], scalar=nega[:, i : i + 1], in1=zs[(v, i)][:], op0=MULT, op1=ADD
+            )
+            nc.sync.dma_start(out=out[P * i : P * (i + 1), 512 * v : 512 * (v + 1)], in_=o[:])
+
+        load_x(0, 0)
+        nc.gpsimd.memset(warm[:], 0.0)
+        nc.scalar.activation(out=warm[:, 0:1], in_=warm[:, 1:2], func=RELU)
+        nc.vector.memset(w1sr[0][:].bitcast(I32), 0)
+        nc.vector.memset(w1sr[1][:].bitcast(I32), 0)
+        nc.vector.memset(w2s[:].bitcast(I32), 0)
+        make_identity(nc, ident[:])
+        nc.gpsimd.memset(af[:], 0.0)
+        load_w1(0, 0)
+        load_w1s(0)
+        load_w1(0, 1)
+        load_x(0, 1)
+        load_x(0, 2)
+        load_x(0, 3)
+        load_w1s(1)
+        load_w1(1, 0)
+        load_w1(1, 1)
+        for i in range(4):
+            load_x(1, i)
+        load_w2s(0, 1024)
+        load_w2(0, 0)
+        load_w2(1, 0)
+        load_w2s(1024, V)
+        load_w2(0, 1)
+        load_w2(1, 1)
+        load_w2(0, 2)
+        load_w2(1, 2)
+        nc.scalar.dma_start(out=abf[0:4, :], in_=alpha.rearrange("(i p) -> i p", p=P))
+
+        b00 = tx(0, 0)
+        cx(0, 0, b00)
+        perm_codes(0, 0, 0)
+        perm_codes(0, 0, 1)
+        qx0(0)
+        perm_scales(0, 0)
+        b01 = tx(0, 1)
+        cx(0, 1, b01)
+        h = s1a(0, 0)
+        r1a(0, 0, h)
+        perm_codes(0, 1, 0)
+        qx0(1)
+        perm_codes(0, 1, 1)
+        perm_scales(0, 1)
+        h = s1a(1, 0)
+        r1a(1, 0, h)
+        b02 = tx(0, 2)
+        cx(0, 2, b02)
+        b03 = tx(0, 3)
+        cx(0, 3, b03)
+        qx0(2)
+        h = s1a(0, 1)
+        r1a(0, 1, h)
+        qx0(3)
+        h = s1a(1, 1)
+        r1a(1, 1, h)
+        perm_codes(1, 0, 0)
+        qh0(0)
+        h = s1a(2, 0)
+        r1a(2, 0, h)
+        perm_codes(1, 0, 1)
+        qh0(1)
+        h = s1a(2, 1)
+        r1a(2, 1, h)
+        perm_scales(1, 0)
+        h = s1a(3, 0)
+        r1a(3, 0, h)
+        b10 = tx(1, 0)
+        cx(1, 0, b10)
+        b11 = tx(1, 1)
+        cx(1, 1, b11)
+        qh0(2)
+        h = s1a(3, 1)
+        r1a(3, 1, h)
+        perm_codes(1, 1, 0)
+        b12 = tx(1, 2)
+        cx(1, 2, b12)
+        b13 = tx(1, 3)
+        cx(1, 3, b13)
+        nc.scalar.activation(out=af[0:4, :], in_=abf[0:4, :], func=COPY, scale=-1.0)
+        ba = bank()
+        nc.tensor.transpose(ba[:, 0:P], af[:], ident[:])
+        qh0(3)
+        perm_codes(1, 1, 1)
+        perm_scales(1, 1)
+        qx1(0)
+        qx1(1)
+        nc.vector.tensor_copy(out=nega[:], in_=ba[:, 0:4])
+
+        order = [(v, i) for v in range(6) for i in range(4)]
+        done0 = 0
+        for k in range(4):
+            z0(*order[k])
+        done0 = 4
+        for G in range(2):
+            for t in range(4):
+                b = s1b(G, t)
+                r1b(G, t, b, "v" if t in (1, 3) else "s")
+            il(G)
+            qh1(G)
+        for k in range(done0, 10):
+            z0(*order[k])
+        done0 = 10
+        done1 = 0
+        while done1 < 24:
+            z1(*order[done1])
+            done1 += 1
+            lead = done0 - done1
+            if done0 < 24 and (lead <= 2 or done1 % 2 == 0):
+                z0(*order[done0])
+                done0 += 1

@@ -24,7 +24,7 @@ def tile_contrastive_decoding_logits_s14_kernel(tc, x, w1_words, w1_scales, w2_w
     nc = tc.nc
     with ExitStack() as ctx:
         keep = ctx.enter_context(tc.tile_pool(name="keep", bufs=1))
-        zpool = ctx.enter_context(tc.tile_pool(name="zpool", bufs=14))
+        zpool = ctx.enter_context(tc.tile_pool(name="zpool", bufs=18))
         opool = ctx.enter_context(tc.tile_pool(name="opool", bufs=6))
         psum = ctx.enter_context(tc.psum_pool(name="psum", bufs=8))
         ctx.enter_context(tc.manual_schedule())
@@ -41,6 +41,7 @@ def tile_contrastive_decoding_logits_s14_kernel(tc, x, w1_words, w1_scales, w2_w
         xg0 = [sb("xg0_%d" % i, [P, 2, P, 4], BF16) for i in range(4)]
         xq0 = [sb("xq0_%d" % i, [P, 2, P], U32) for i in range(4)]
         xqs0 = [sb("xqs0_%d" % i, [P, 2, P], U8) for i in range(4)]
+        xe = [sb("xe_%d" % i, [P, 2, 2, P], F32) for i in range(4)]
         xg1 = sb("xg1", [P, 2, T, 4], BF16)
         xq1 = [sb("xq1_%d" % g, [P, T], U32) for g in range(2)]
         xqs1 = [sb("xqs1_%d" % g, [P, T], U8) for g in range(2)]
@@ -119,10 +120,30 @@ def tile_contrastive_decoding_logits_s14_kernel(tc, x, w1_words, w1_scales, w2_w
                 in_=xg1[:, g, :, :].rearrange("p r f -> p (r f)"),
             )
 
-        def perm_codes(m, G, g):
+        def de1(i):
             nc.vector.tensor_copy(
-                out=w1p[m][:, G, g, :, :].rearrange("p t (m e) -> p t m e", e=2),
-                in_=w1r[m][:, G, g, :].rearrange("p (m t e) -> p t m e", t=4, e=2),
+                out=xe[i][:],
+                in_=xs[1][i][:].bitcast(F32).rearrange("p (g q u) -> p g u q", g=2, u=2),
+            )
+
+        def tx1(i, eng):
+            b = bank()
+            bv = b[:].rearrange("p (g u r) -> p g u r", g=2, u=2)
+            for g in range(2):
+                for u in range(2):
+                    nc.tensor.transpose(bv[:, g, u, :], xe[i][:, g, u, :], ident[:])
+            words = xg1[:].rearrange("p g r f -> p (g r f)").bitcast(F32).rearrange("p (g r u) -> p g r u", g=2, u=2)
+            dst = words[:, :, P * i : P * (i + 1), :]
+            src = bv.rearrange("p g u r -> p g r u")
+            if eng == "s":
+                nc.scalar.copy(out=dst, in_=src)
+            else:
+                nc.vector.tensor_copy(out=dst, in_=src)
+
+        def perm_codes(m, G, t):
+            nc.vector.tensor_copy(
+                out=w1p[m][:, G, :, t, :].rearrange("p g (m e) -> p g m e", e=2),
+                in_=w1r[m][:, G, :, :].rearrange("p g (m t e) -> p g t m e", t=4, e=2)[:, :, t, :, :],
             )
 
         def perm_scales(m, G):
@@ -232,7 +253,34 @@ def tile_contrastive_decoding_logits_s14_kernel(tc, x, w1_words, w1_scales, w2_w
             )
             nc.sync.dma_start(out=out[P * i : P * (i + 1), 512 * v : 512 * (v + 1)], in_=o[:])
 
+        def z1_last(v, i):
+            o = opool.tile([P, 512], F32, name="o")
+            for half in range(2):
+                b = bank()
+                for quarter in (2 * half, 2 * half + 1):
+                    c = P * (quarter - 2 * half)
+                    for G in range(2):
+                        lo = 1024 * (v % 2) + 256 * quarter
+                        nlo = 512 * v + P * quarter
+                        nc.tensor.matmul_mx(
+                            out=b[:, c : c + P],
+                            lhsT=hq1[G][:, P * i : P * (i + 1)].bitcast(FP8X4),
+                            lhsT_scale=hqs1[G][:, P * i : P * (i + 1)],
+                            rhs=w2t[1][v // 2][:, G, lo : lo + 256].bitcast(FP4X4),
+                            rhs_scale=w2s[:, 2 + G, nlo : nlo + P],
+                            start=(G == 0),
+                            stop=(G == 1),
+                        )
+                cols = slice(256 * half, 256 * (half + 1))
+                nc.vector.scalar_tensor_tensor(
+                    out=o[:, cols], in0=b[:, 0:256], scalar=nega[:, i : i + 1], in1=zs[(v, i)][:, cols], op0=MULT, op1=ADD
+                )
+                nc.sync.dma_start(
+                    out=out[P * i : P * (i + 1), 512 * v + 256 * half : 512 * v + 256 * (half + 1)], in_=o[:, cols]
+                )
+
         load_x(0, 0)
+        load_w1(0, 0)
         nc.gpsimd.memset(warm[:], 0.0)
         nc.scalar.activation(out=warm[:, 0:1], in_=warm[:, 1:2], func=RELU)
         nc.vector.memset(w1sr[0][:].bitcast(I32), 0)
@@ -240,17 +288,16 @@ def tile_contrastive_decoding_logits_s14_kernel(tc, x, w1_words, w1_scales, w2_w
         nc.vector.memset(w2s[:].bitcast(I32), 0)
         make_identity(nc, ident[:])
         nc.gpsimd.memset(af[:], 0.0)
-        load_w1(0, 0)
         load_w1s(0)
-        load_w1(0, 1)
         load_x(0, 1)
         load_x(0, 2)
+        load_w1(0, 1)
         load_x(0, 3)
+        for i in range(4):
+            load_x(1, i)
         load_w1s(1)
         load_w1(1, 0)
         load_w1(1, 1)
-        for i in range(4):
-            load_x(1, i)
         load_w2s(0, 1024)
         load_w2(0, 0)
         load_w2(1, 0)
@@ -261,84 +308,80 @@ def tile_contrastive_decoding_logits_s14_kernel(tc, x, w1_words, w1_scales, w2_w
         load_w2(1, 2)
         nc.scalar.dma_start(out=abf[0:4, :], in_=alpha.rearrange("(i p) -> i p", p=P))
 
-        b00 = tx(0, 0)
-        cx(0, 0, b00)
+        def tc_x(i):
+            cx(0, i, tx(0, i))
+
+        def sr_a(i, G):
+            r1a(i, G, s1a(i, G))
+
+        tc_x(0)
         perm_codes(0, 0, 0)
         perm_codes(0, 0, 1)
-        qx0(0)
         perm_scales(0, 0)
-        b01 = tx(0, 1)
-        cx(0, 1, b01)
-        h = s1a(0, 0)
-        r1a(0, 0, h)
-        perm_codes(0, 1, 0)
+        qx0(0)
+        perm_codes(0, 0, 2)
+        perm_codes(0, 0, 3)
+        tc_x(1)
+        tc_x(2)
+        sr_a(0, 0)
         qx0(1)
+        perm_codes(0, 1, 0)
+        qx0(2)
         perm_codes(0, 1, 1)
         perm_scales(0, 1)
-        h = s1a(1, 0)
-        r1a(1, 0, h)
-        b02 = tx(0, 2)
-        cx(0, 2, b02)
-        b03 = tx(0, 3)
-        cx(0, 3, b03)
-        qx0(2)
-        h = s1a(0, 1)
-        r1a(0, 1, h)
+        perm_codes(0, 1, 2)
+        perm_codes(0, 1, 3)
+        sr_a(1, 0)
+        sr_a(2, 0)
+        de1(0)
+        de1(1)
+        sr_a(0, 1)
+        sr_a(1, 1)
+        tc_x(3)
+        de1(2)
+        de1(3)
+        tx1(0, "s")
+        tx1(1, "v")
         qx0(3)
-        h = s1a(1, 1)
-        r1a(1, 1, h)
-        perm_codes(1, 0, 0)
-        qh0(0)
-        h = s1a(2, 0)
-        r1a(2, 0, h)
-        perm_codes(1, 0, 1)
-        qh0(1)
-        h = s1a(2, 1)
-        r1a(2, 1, h)
-        perm_scales(1, 0)
-        h = s1a(3, 0)
-        r1a(3, 0, h)
-        b10 = tx(1, 0)
-        cx(1, 0, b10)
-        b11 = tx(1, 1)
-        cx(1, 1, b11)
-        qh0(2)
-        h = s1a(3, 1)
-        r1a(3, 1, h)
-        perm_codes(1, 1, 0)
-        b12 = tx(1, 2)
-        cx(1, 2, b12)
-        b13 = tx(1, 3)
-        cx(1, 3, b13)
+        tx1(2, "s")
+        tx1(3, "v")
         nc.scalar.activation(out=af[0:4, :], in_=abf[0:4, :], func=COPY, scale=-1.0)
         ba = bank()
         nc.tensor.transpose(ba[:, 0:P], af[:], ident[:])
-        qh0(3)
-        perm_codes(1, 1, 1)
-        perm_scales(1, 1)
+        nc.vector.tensor_copy(out=nega[:], in_=ba[:, 0:4])
+        sr_a(2, 1)
+        sr_a(3, 0)
+        sr_a(3, 1)
+        qh0(0)
+        qh0(1)
+        qh0(2)
+        for t in range(4):
+            perm_codes(1, 0, t)
+        perm_scales(1, 0)
         qx1(0)
         qx1(1)
-        nc.vector.tensor_copy(out=nega[:], in_=ba[:, 0:4])
-
-        order = [(v, i) for v in range(6) for i in range(4)]
-        done0 = 0
-        for k in range(4):
+        qh0(3)
+        for t in range(4):
+            perm_codes(1, 1, t)
+        perm_scales(1, 1)
+        order = [(0, 0), (0, 1), (1, 0), (1, 1), (0, 2), (1, 2), (0, 3), (1, 3)]
+        order += [(v, i) for v in range(2, 6) for i in range(4)]
+        for k in range(6):
             z0(*order[k])
-        done0 = 4
         for G in range(2):
             for t in range(4):
                 b = s1b(G, t)
-                r1b(G, t, b, "v" if t in (1, 3) else "s")
+                r1b(G, t, b, "v" if (t % 2 == 1 and G == 0) else "s")
             il(G)
             qh1(G)
-        for k in range(done0, 10):
+        for k in range(6, 14):
             z0(*order[k])
-        done0 = 10
-        done1 = 0
-        while done1 < 24:
-            z1(*order[done1])
-            done1 += 1
-            lead = done0 - done1
-            if done0 < 24 and (lead <= 2 or done1 % 2 == 0):
+        done0 = 14
+        for k in range(24):
+            if k < 23:
+                z1(*order[k])
+            else:
+                z1_last(*order[k])
+            if done0 < 24 and done0 - (k + 1) <= 3:
                 z0(*order[done0])
                 done0 += 1

@@ -37,20 +37,24 @@ def tile_contrastive_decoding_logits_s14_kernel(tc, x, w1_words, w1_scales, w2_w
             t = keep.tile(shape, dt, name=name, align_bytes=256)
             return t
 
-        xs = [[sb("x%d_%d" % (m, i), [P, K], BF16) for i in range(4)] for m in range(2)]
+        x0a = [sb("x0a_%d" % i, [P, K], BF16) for i in range(2)]
+        x0b = sb("x0b", [P, 2, K], BF16)
+        x1 = [sb("x1_%d" % h, [P, 2, K], BF16) for h in range(2)]
+        xe0 = [sb("xe0_%d" % i, [P, 2, 2, P], F32) for i in range(2)]
+        xe1 = [sb("xe1_%d" % i, [P, 2, 2, P], F32) for i in range(4)]
         xg0 = [sb("xg0_%d" % i, [P, 2, P, 4], BF16) for i in range(4)]
         xq0 = [sb("xq0_%d" % i, [P, 2, P], U32) for i in range(4)]
         xqs0 = [sb("xqs0_%d" % i, [P, 2, P], U8) for i in range(4)]
-        xe = [sb("xe_%d" % i, [P, 2, 2, P], F32) for i in range(4)]
         xg1 = sb("xg1", [P, 2, T, 4], BF16)
         xq1 = [sb("xq1_%d" % g, [P, T], U32) for g in range(2)]
         xqs1 = [sb("xqs1_%d" % g, [P, T], U8) for g in range(2)]
-        w1r = [sb("w1r%d" % m, [P, 2, 2, 1024], U8) for m in range(2)]
-        w1p = [sb("w1p%d" % m, [P, 2, 2, 4, 256], U8) for m in range(2)]
+        w1r = [sb("w1r%d" % m, [P, 2, 2048], U8) for m in range(2)]
         w1sr = [sb("w1sr%d" % m, [P, 2, 1024], U8) for m in range(2)]
-        w1sp = [sb("w1sp%d" % m, [P, 2, 2, 512], U8) for m in range(2)]
+        w1p = sb("w1p", [P, 2, 2, 4, 256], U8)
+        w1sp = sb("w1sp", [P, 2, 2, 512], U8)
         w2t = [[sb("w2_%d_%d" % (m, vp), [P, 2, 2048], U8) for vp in range(3)] for m in range(2)]
-        w2s = sb("w2s", [P, 4, V], U8)
+        w2s = [sb("w2s%d" % m, [P, 2, V], U8) for m in range(2)]
+        he = [sb("he_%d" % i, [P, 2, 2, P, 2], BF16) for i in range(4)]
         hb0 = [sb("hb0_%d" % i, [P, 2, P, 4], BF16) for i in range(4)]
         hq0 = [sb("hq0_%d" % i, [P, 2, P], U32) for i in range(4)]
         hqs0 = [sb("hqs0_%d" % i, [P, 2, P], U8) for i in range(4)]
@@ -64,19 +68,16 @@ def tile_contrastive_decoding_logits_s14_kernel(tc, x, w1_words, w1_scales, w2_w
         nega = sb("nega", [P, 4], F32)
         warm = sb("warm", [P, 2], F32)
 
-        def load_x(m, i):
-            nc.sync.dma_start(out=xs[m][i][:], in_=x[m, P * i : P * (i + 1), :])
-
-        def load_w1(m, G):
+        def load_w1(m, lo, hi):
             nc.sync.dma_start(
-                out=w1r[m][:, G, :, :].bitcast(I32),
-                in_=w1_words[2 * m : 2 * m + 2, :, 1024 * G : 1024 * (G + 1)].rearrange("g p c -> p g c").bitcast(I32),
+                out=w1r[m][:, :, lo:hi].bitcast(I32),
+                in_=w1_words[2 * m : 2 * m + 2, :, lo:hi].rearrange("g p c -> p g c").bitcast(I32),
             )
 
-        def load_w1s(m):
-            src = w1_scales[2 * m : 2 * m + 2].rearrange("g (q r) n -> r q g n", r=4)
+        def load_scales(tile, dram, m):
+            src = dram[2 * m : 2 * m + 2].rearrange("g (q r) n -> r q g n", r=4)
             for r in range(4):
-                nc.sync.dma_start(out=w1sr[m][r:P:32, :, :].bitcast(I32), in_=src[r].bitcast(I32))
+                nc.sync.dma_start(out=tile[r:P:32, :, :].bitcast(I32), in_=src[r].bitcast(I32))
 
         def load_w2(m, vp):
             nc.sync.dma_start(
@@ -84,304 +85,250 @@ def tile_contrastive_decoding_logits_s14_kernel(tc, x, w1_words, w1_scales, w2_w
                 in_=w2_words[2 * m : 2 * m + 2, :, 2048 * vp : 2048 * (vp + 1)].rearrange("g p c -> p g c").bitcast(I32),
             )
 
-        def load_w2s(lo, hi):
-            src = w2_scales.rearrange("g (q r) n -> r q g n", r=4)
-            for r in range(4):
-                nc.sync.dma_start(out=w2s[r:P:32, :, lo:hi].bitcast(I32), in_=src[r][:, :, lo:hi].bitcast(I32))
+        def load_pair(tile, m, h):
+            nc.sync.dma_start(out=tile[:], in_=x[m, 256 * h : 256 * (h + 1), :].rearrange("(i p) k -> p i k", i=2))
 
-        def tx(m, i):
+        def move(eng, out, in_):
+            if eng == "s":
+                nc.scalar.copy(out=out, in_=in_)
+            else:
+                nc.vector.tensor_copy(out=out, in_=in_)
+
+        def relu(eng, out, in_):
+            if eng == "s":
+                nc.scalar.activation(out=out, in_=in_, func=RELU)
+            else:
+                nc.vector.tensor_scalar_max(out=out, in0=in_, scalar1=0.0)
+
+        def turn(srcs):
             b = bank()
             bv = b[:].rearrange("p (g u r) -> p g u r", g=2, u=2)
-            words = xs[m][i][:].bitcast(F32)
             for g in range(2):
                 for u in range(2):
-                    nc.tensor.transpose(bv[:, g, u, :], words[:, 256 * g + u : 256 * (g + 1) : 2], ident[:])
-            return bv
+                    nc.tensor.transpose(bv[:, g, u, :], srcs(g, u), ident[:])
+            return bv.rearrange("p g u r -> p g r u")
 
-        def cx(m, i, bv):
-            src = bv.rearrange("p g u r -> p g r u")
-            if m == 0:
-                dst = xg0[i][:].rearrange("p g r f -> p (g r f)").bitcast(F32).rearrange("p (g r u) -> p g r u", g=2, u=2)
+        def words(t):
+            return t.rearrange("p g r f -> p (g r f)").bitcast(F32).rearrange("p (g r u) -> p g r u", g=2, u=2)
+
+        def deint(dst, x_tile):
+            nc.vector.tensor_copy(out=dst[:], in_=x_tile.bitcast(F32).rearrange("p (g q u) -> p g u q", g=2, u=2))
+
+        def tx0(i, eng):
+            if i < 2:
+                wd = x0a[i][:].bitcast(F32)
+                bv = turn(lambda g, u: wd[:, 256 * g + u : 256 * (g + 1) : 2])
             else:
-                dst = xg1[:].rearrange("p g r f -> p (g r f)").bitcast(F32).rearrange("p (g r u) -> p g r u", g=2, u=2)[:, :, P * i : P * (i + 1), :]
-            nc.scalar.copy(out=dst, in_=src)
+                bv = turn(lambda g, u: xe0[i - 2][:, g, u, :])
+            move(eng, words(xg0[i][:]), bv)
+
+        def tx1(i, eng):
+            bv = turn(lambda g, u: xe1[i][:, g, u, :])
+            move(eng, words(xg1[:])[:, :, P * i : P * (i + 1), :], bv)
+
+        def th(i, eng):
+            bv = turn(lambda g, u: he[i][:, g, u, :, :].rearrange("r p e -> r (p e)").bitcast(F32))
+            move(eng, words(hb0[i][:]), bv)
+
+        def quant(codes, scales, src):
+            nc.vector.quantize_mx(out=codes.bitcast(FP8X4), scales=scales, in_=src)
 
         def qx0(i):
-            nc.vector.quantize_mx(
-                out=xq0[i][:].rearrange("p g r -> p (g r)").bitcast(FP8X4),
-                scales=xqs0[i][:].rearrange("p g r -> p (g r)"),
-                in_=xg0[i][:].rearrange("p g r f -> p (g r f)"),
+            quant(
+                xq0[i][:].rearrange("p g r -> p (g r)"),
+                xqs0[i][:].rearrange("p g r -> p (g r)"),
+                xg0[i][:].rearrange("p g r f -> p (g r f)"),
+            )
+
+        def qh0(i):
+            quant(
+                hq0[i][:].rearrange("p g r -> p (g r)"),
+                hqs0[i][:].rearrange("p g r -> p (g r)"),
+                hb0[i][:].rearrange("p g r f -> p (g r f)"),
             )
 
         def qx1(g):
-            nc.vector.quantize_mx(
-                out=xq1[g][:].bitcast(FP8X4),
-                scales=xqs1[g][:],
-                in_=xg1[:, g, :, :].rearrange("p r f -> p (r f)"),
-            )
+            quant(xq1[g][:], xqs1[g][:], xg1[:, g, :, :].rearrange("p r f -> p (r f)"))
 
-        def de1(i):
+        def qh1(g):
+            quant(hq1[g][:], hqs1[g][:], hb1[g][:].rearrange("p r f -> p (r f)"))
+
+        def perm_codes(G, t):
             nc.vector.tensor_copy(
-                out=xe[i][:],
-                in_=xs[1][i][:].bitcast(F32).rearrange("p (g q u) -> p g u q", g=2, u=2),
+                out=w1p[:, G, :, t, :].rearrange("p g (m e) -> p g m e", e=2),
+                in_=w1r[1][:, :, 1024 * G : 1024 * (G + 1)].rearrange("p g (m t e) -> p g t m e", t=4, e=2)[:, :, t, :, :],
             )
 
-        def tx1(i, eng):
-            b = bank()
-            bv = b[:].rearrange("p (g u r) -> p g u r", g=2, u=2)
-            for g in range(2):
-                for u in range(2):
-                    nc.tensor.transpose(bv[:, g, u, :], xe[i][:, g, u, :], ident[:])
-            words = xg1[:].rearrange("p g r f -> p (g r f)").bitcast(F32).rearrange("p (g r u) -> p g r u", g=2, u=2)
-            dst = words[:, :, P * i : P * (i + 1), :]
-            src = bv.rearrange("p g u r -> p g r u")
-            if eng == "s":
-                nc.scalar.copy(out=dst, in_=src)
-            else:
-                nc.vector.tensor_copy(out=dst, in_=src)
-
-        def perm_codes(m, G, t):
+        def perm_scales(G):
             nc.vector.tensor_copy(
-                out=w1p[m][:, G, :, t, :].rearrange("p g (m e) -> p g m e", e=2),
-                in_=w1r[m][:, G, :, :].rearrange("p g (m t e) -> p g t m e", t=4, e=2)[:, :, t, :, :],
+                out=w1sp[:, G, :, :].rearrange("p g (t m) -> p g t m", t=4),
+                in_=w1sr[1][:, :, 512 * G : 512 * (G + 1)].rearrange("p g (m t) -> p g t m", t=4),
             )
 
-        def perm_scales(m, G):
-            nc.vector.tensor_copy(
-                out=w1sp[m][:, G, :, :].rearrange("p g (t m) -> p g t m", t=4),
-                in_=w1sr[m][:, :, 512 * G : 512 * (G + 1)].rearrange("p g (m t) -> p g t m", t=4),
+        def mm(b, lhsT, lhsT_scale, rhs, rhs_scale, g):
+            nc.tensor.matmul_mx(
+                out=b, lhsT=lhsT, lhsT_scale=lhsT_scale, rhs=rhs, rhs_scale=rhs_scale, start=(g == 0), stop=(g == 1)
             )
 
-        def s1a(i, G):
-            b = bank()
-            bv = b[:].rearrange("p (t r) -> p t r", t=4)
-            for t in range(4):
-                for g in range(2):
-                    nc.tensor.matmul_mx(
-                        out=bv[:, t, :],
-                        lhsT=w1p[0][:, G, g, t, :].bitcast(FP4X4),
-                        lhsT_scale=w1sp[0][:, G, g, P * t : P * (t + 1)],
-                        rhs=xq0[i][:, g, :].bitcast(FP8X4),
-                        rhs_scale=xqs0[i][:, g, :],
-                        start=(g == 0),
-                        stop=(g == 1),
-                    )
-            return bv
-
-        def r1a(i, G, bv):
-            nc.scalar.activation(out=hb0[i][:, G, :, :], in_=bv.rearrange("p t r -> p r t"), func=RELU)
-
-        def qh0(i):
-            nc.vector.quantize_mx(
-                out=hq0[i][:].rearrange("p g r -> p (g r)").bitcast(FP8X4),
-                scales=hqs0[i][:].rearrange("p g r -> p (g r)"),
-                in_=hb0[i][:].rearrange("p g r f -> p (g r f)"),
-            )
-
-        def s1b(G, t):
+        def s1h(i, G, eng):
             b = bank()
             for g in range(2):
-                nc.tensor.matmul_mx(
-                    out=b[:],
-                    lhsT=w1p[1][:, G, g, t, :].bitcast(FP4X4),
-                    lhsT_scale=w1sp[1][:, G, g, P * t : P * (t + 1)],
-                    rhs=xq1[g][:].bitcast(FP8X4),
-                    rhs_scale=xqs1[g][:],
-                    start=(g == 0),
-                    stop=(g == 1),
+                mm(
+                    b[:],
+                    xq0[i][:, g, :].bitcast(FP8X4),
+                    xqs0[i][:, g, :],
+                    w1r[0][:, g, 1024 * G : 1024 * (G + 1)].bitcast(FP4X4),
+                    w1sr[0][:, g, 512 * G : 512 * (G + 1)],
+                    g,
                 )
-            return b
+            relu(eng, he[i][:, G, :, :, :], b[:].rearrange("r (p u e) -> r u p e", u=2, e=2))
 
-        def r1b(G, t, b, eng):
-            if eng == "s":
-                nc.scalar.activation(out=hr1[G][:, t, :], in_=b[:], func=RELU)
-            else:
-                nc.vector.tensor_scalar_max(out=hr1[G][:, t, :], in0=b[:], scalar1=0.0)
+        def s1b(G, t, eng):
+            b = bank()
+            for g in range(2):
+                mm(
+                    b[:],
+                    w1p[:, G, g, t, :].bitcast(FP4X4),
+                    w1sp[:, G, g, P * t : P * (t + 1)],
+                    xq1[g][:].bitcast(FP8X4),
+                    xqs1[g][:],
+                    g,
+                )
+            relu(eng, hr1[G][:, t, :], b[:])
 
         def il(G):
             nc.vector.tensor_copy(out=hb1[G][:], in_=hr1[G][:].rearrange("p t r -> p r t"))
 
-        def qh1(G):
-            nc.vector.quantize_mx(
-                out=hq1[G][:].bitcast(FP8X4),
-                scales=hqs1[G][:],
-                in_=hb1[G][:].rearrange("p r f -> p (r f)"),
-            )
-
         zs = {}
-
-        def w2_args(m, v, G):
-            lo = 1024 * (v % 2)
-            return (
-                w2t[m][v // 2][:, G, lo : lo + 1024].bitcast(FP4X4),
-                w2s[:, 2 * m + G, 512 * v : 512 * (v + 1)],
-            )
 
         def z0(v, i):
             b = bank()
+            lo = 1024 * (v % 2)
             for G in range(2):
-                rhs, rhs_scale = w2_args(0, v, G)
-                nc.tensor.matmul_mx(
-                    out=b[:],
-                    lhsT=hq0[i][:, G, :].bitcast(FP8X4),
-                    lhsT_scale=hqs0[i][:, G, :],
-                    rhs=rhs,
-                    rhs_scale=rhs_scale,
-                    start=(G == 0),
-                    stop=(G == 1),
+                mm(
+                    b[:],
+                    hq0[i][:, G, :].bitcast(FP8X4),
+                    hqs0[i][:, G, :],
+                    w2t[0][v // 2][:, G, lo : lo + 1024].bitcast(FP4X4),
+                    w2s[0][:, G, 512 * v : 512 * (v + 1)],
+                    G,
                 )
             z = zpool.tile([P, 512], F32, name="z")
             nc.scalar.copy(out=z[:], in_=b[:])
             zs[(v, i)] = z
 
-        def z1(v, i):
-            b = bank()
-            for G in range(2):
-                rhs, rhs_scale = w2_args(1, v, G)
-                nc.tensor.matmul_mx(
-                    out=b[:],
-                    lhsT=hq1[G][:, P * i : P * (i + 1)].bitcast(FP8X4),
-                    lhsT_scale=hqs1[G][:, P * i : P * (i + 1)],
-                    rhs=rhs,
-                    rhs_scale=rhs_scale,
-                    start=(G == 0),
-                    stop=(G == 1),
-                )
+        def z1(v, i, parts):
             o = opool.tile([P, 512], F32, name="o")
-            nc.vector.scalar_tensor_tensor(
-                out=o[:], in0=b[:], scalar=nega[:, i : i + 1], in1=zs[(v, i)][:], op0=MULT, op1=ADD
-            )
-            nc.sync.dma_start(out=out[P * i : P * (i + 1), 512 * v : 512 * (v + 1)], in_=o[:])
-
-        def z1_last(v, i):
-            o = opool.tile([P, 512], F32, name="o")
-            for half in range(2):
+            toks = slice(P * i, P * (i + 1))
+            for part in range(parts):
                 b = bank()
-                for quarter in (2 * half, 2 * half + 1):
-                    c = P * (quarter - 2 * half)
+                w = 512 // parts
+                n = 512 if parts == 1 else P
+                for c in range(0, w, n):
+                    col = part * w + c
+                    lo = 1024 * (v % 2) + 2 * col
                     for G in range(2):
-                        lo = 1024 * (v % 2) + 256 * quarter
-                        nlo = 512 * v + P * quarter
-                        nc.tensor.matmul_mx(
-                            out=b[:, c : c + P],
-                            lhsT=hq1[G][:, P * i : P * (i + 1)].bitcast(FP8X4),
-                            lhsT_scale=hqs1[G][:, P * i : P * (i + 1)],
-                            rhs=w2t[1][v // 2][:, G, lo : lo + 256].bitcast(FP4X4),
-                            rhs_scale=w2s[:, 2 + G, nlo : nlo + P],
-                            start=(G == 0),
-                            stop=(G == 1),
+                        mm(
+                            b[:, c : c + n],
+                            hq1[G][:, toks].bitcast(FP8X4),
+                            hqs1[G][:, toks],
+                            w2t[1][v // 2][:, G, lo : lo + 2 * n].bitcast(FP4X4),
+                            w2s[1][:, G, 512 * v + col : 512 * v + col + n],
+                            G,
                         )
-                cols = slice(256 * half, 256 * (half + 1))
+                cols = slice(part * w, (part + 1) * w)
                 nc.vector.scalar_tensor_tensor(
-                    out=o[:, cols], in0=b[:, 0:256], scalar=nega[:, i : i + 1], in1=zs[(v, i)][:, cols], op0=MULT, op1=ADD
+                    out=o[:, cols], in0=b[:, 0:w], scalar=nega[:, i : i + 1], in1=zs[(v, i)][:, cols], op0=MULT, op1=ADD
                 )
-                nc.sync.dma_start(
-                    out=out[P * i : P * (i + 1), 512 * v + 256 * half : 512 * v + 256 * (half + 1)], in_=o[:, cols]
-                )
+                nc.sync.dma_start(out=out[toks, 512 * v + part * w : 512 * v + (part + 1) * w], in_=o[:, cols])
 
-        load_x(0, 0)
-        load_w1(0, 0)
+        nc.sync.dma_start(out=x0a[0][:], in_=x[0, 0:P, :])
+        load_w1(0, 0, 1024)
         nc.gpsimd.memset(warm[:], 0.0)
+        nc.scalar.dma_start(out=abf[0:4, :], in_=alpha.rearrange("(i p) -> i p", p=P))
         nc.scalar.activation(out=warm[:, 0:1], in_=warm[:, 1:2], func=RELU)
-        nc.vector.memset(w1sr[0][:].bitcast(I32), 0)
-        nc.vector.memset(w1sr[1][:].bitcast(I32), 0)
-        nc.vector.memset(w2s[:].bitcast(I32), 0)
+        for t in (w1sr[0], w1sr[1], w2s[0], w2s[1]):
+            nc.vector.memset(t[:].bitcast(I32), 0)
         make_identity(nc, ident[:])
         nc.gpsimd.memset(af[:], 0.0)
-        load_w1s(0)
-        load_x(0, 1)
-        load_x(0, 2)
-        load_w1(0, 1)
-        load_x(0, 3)
-        for i in range(4):
-            load_x(1, i)
-        load_w1s(1)
-        load_w1(1, 0)
-        load_w1(1, 1)
-        load_w2s(0, 1024)
+        load_scales(w1sr[0], w1_scales, 0)
+        nc.sync.dma_start(out=x0a[1][:], in_=x[0, P : 2 * P, :])
+        load_w1(0, 1024, 2048)
+        load_pair(x0b, 0, 1)
+        load_scales(w1sr[1], w1_scales, 1)
+        load_w1(1, 0, 2048)
+        load_pair(x1[0], 1, 0)
+        load_pair(x1[1], 1, 1)
+        load_scales(w2s[0], w2_scales, 0)
         load_w2(0, 0)
-        load_w2(1, 0)
-        load_w2s(1024, V)
         load_w2(0, 1)
-        load_w2(1, 1)
         load_w2(0, 2)
-        load_w2(1, 2)
-        nc.scalar.dma_start(out=abf[0:4, :], in_=alpha.rearrange("(i p) -> i p", p=P))
+        load_scales(w2s[1], w2_scales, 1)
+        for vp in range(3):
+            load_w2(1, vp)
 
-        def tc_x(i):
-            cx(0, i, tx(0, i))
-
-        def sr_a(i, G):
-            r1a(i, G, s1a(i, G))
-
-        tc_x(0)
-        perm_codes(0, 0, 0)
-        perm_codes(0, 0, 1)
-        perm_scales(0, 0)
+        tx0(0, "s")
         qx0(0)
-        perm_codes(0, 0, 2)
-        perm_codes(0, 0, 3)
-        tc_x(1)
-        tc_x(2)
-        sr_a(0, 0)
+        tx0(1, "s")
+        s1h(0, 0, "s")
         qx0(1)
-        perm_codes(0, 1, 0)
+        s1h(0, 1, "s")
+        for i in range(2):
+            deint(xe0[i], x0b[:, i, :])
+        tx0(2, "s")
+        tx0(3, "v")
         qx0(2)
-        perm_codes(0, 1, 1)
-        perm_scales(0, 1)
-        perm_codes(0, 1, 2)
-        perm_codes(0, 1, 3)
-        sr_a(1, 0)
-        sr_a(2, 0)
-        de1(0)
-        de1(1)
-        sr_a(0, 1)
-        sr_a(1, 1)
-        tc_x(3)
-        de1(2)
-        de1(3)
-        tx1(0, "s")
-        tx1(1, "v")
         qx0(3)
-        tx1(2, "s")
-        tx1(3, "v")
+        for t in range(3):
+            perm_codes(0, t)
+        for i in (1, 2, 3):
+            s1h(i, 0, "s")
+            s1h(i, 1, "s" if i == 1 else "v")
+            if i == 2:
+                perm_codes(0, 3)
+                for j in range(2):
+                    deint(xe1[j], x1[0][:, j, :])
+        for j in range(2):
+            deint(xe1[2 + j], x1[1][:, j, :])
+        th(0, "s")
+        th(1, "s")
+        th(2, "v")
+        qh0(0)
+        tx1(0, "s")
+        qh0(1)
+        tx1(1, "s")
+        qh0(2)
+        th(3, "s")
+        tx1(2, "v")
+        qh0(3)
+        tx1(3, "s")
         nc.scalar.activation(out=af[0:4, :], in_=abf[0:4, :], func=COPY, scale=-1.0)
         ba = bank()
         nc.tensor.transpose(ba[:, 0:P], af[:], ident[:])
         nc.vector.tensor_copy(out=nega[:], in_=ba[:, 0:4])
-        sr_a(2, 1)
-        sr_a(3, 0)
-        sr_a(3, 1)
-        qh0(0)
-        qh0(1)
-        qh0(2)
-        for t in range(4):
-            perm_codes(1, 0, t)
-        perm_scales(1, 0)
+        perm_scales(0)
         qx1(0)
         qx1(1)
-        qh0(3)
+        perm_scales(1)
         for t in range(4):
-            perm_codes(1, 1, t)
-        perm_scales(1, 1)
-        order = [(0, 0), (0, 1), (1, 0), (1, 1), (0, 2), (1, 2), (0, 3), (1, 3)]
+            perm_codes(1, t)
+
+        order = [(v, i) for v in range(2) for i in range(3)] + [(0, 3), (1, 3)]
         order += [(v, i) for v in range(2, 6) for i in range(4)]
-        for k in range(6):
+        for k in range(8):
             z0(*order[k])
         for G in range(2):
             for t in range(4):
-                b = s1b(G, t)
-                r1b(G, t, b, "v" if (t % 2 == 1 and G == 0) else "s")
+                s1b(G, t, "v" if (G == 0 and t % 2 == 1) else "s")
             il(G)
             qh1(G)
-        for k in range(6, 14):
+            if G == 0:
+                z0(*order[8])
+        for k in range(9, 16):
             z0(*order[k])
-        done0 = 14
+        done0 = 16
         for k in range(24):
-            if k < 23:
-                z1(*order[k])
-            else:
-                z1_last(*order[k])
+            z1(*order[k], 2 if k == 23 else 1)
             if done0 < 24 and done0 - (k + 1) <= 3:
                 z0(*order[done0])
                 done0 += 1

from contextlib import ExitStack

import concourse.mybir as mybir
from concourse.masks import make_identity

F32 = mybir.dt.float32
BF16 = mybir.dt.bfloat16
U32 = mybir.dt.uint32
I32 = mybir.dt.int32
U8 = mybir.dt.uint8
FP8X4 = mybir.dt.float8_e4m3fn_x4
FP4X4 = mybir.dt.float4_e2m1fn_x4
RELU = mybir.ActivationFunctionType.Relu
COPY = mybir.ActivationFunctionType.Copy
MULT = mybir.AluOpType.mult
ADD = mybir.AluOpType.add

T, K, F, V = 512, 1024, 1024, 3072
P = 128
FLOPS = 2 * 2 * T * K * F + 2 * 2 * T * F * V


def tile_contrastive_decoding_logits_s14_kernel(tc, x, w1_words, w1_scales, w2_words, w2_scales, alpha, out):
    nc = tc.nc
    with ExitStack() as ctx:
        keep = ctx.enter_context(tc.tile_pool(name="keep", bufs=1))
        zpool = ctx.enter_context(tc.tile_pool(name="zpool", bufs=18))
        opool = ctx.enter_context(tc.tile_pool(name="opool", bufs=6))
        psum = ctx.enter_context(tc.psum_pool(name="psum", bufs=8))
        ctx.enter_context(tc.manual_schedule())

        def bank():
            b = psum.tile([P, 512], F32, name="bank")
            return b

        def sb(name, shape, dt):
            t = keep.tile(shape, dt, name=name, align_bytes=256)
            return t

        x0a = [sb("x0a_%d" % i, [P, K], BF16) for i in range(2)]
        x0b = sb("x0b", [P, 2, K], BF16)
        x1 = [sb("x1_%d" % h, [P, 2, K], BF16) for h in range(2)]
        xe0 = [sb("xe0_%d" % i, [P, 2, 2, P], F32) for i in range(2)]
        xe1 = [sb("xe1_%d" % i, [P, 2, 2, P], F32) for i in range(4)]
        xg0 = [sb("xg0_%d" % i, [P, 2, P, 4], BF16) for i in range(4)]
        xq0 = [sb("xq0_%d" % i, [P, 2, P], U32) for i in range(4)]
        xqs0 = [sb("xqs0_%d" % i, [P, 2, P], U8) for i in range(4)]
        xg1 = sb("xg1", [P, 2, T, 4], BF16)
        xq1 = [sb("xq1_%d" % g, [P, T], U32) for g in range(2)]
        xqs1 = [sb("xqs1_%d" % g, [P, T], U8) for g in range(2)]
        w1r = [sb("w1r%d" % m, [P, 2, 2048], U8) for m in range(2)]
        w1sr = [sb("w1sr%d" % m, [P, 2, 1024], U8) for m in range(2)]
        w1p = sb("w1p", [P, 2, 2, 4, 256], U8)
        w1sp = sb("w1sp", [P, 2, 2, 512], U8)
        w2t = [[sb("w2_%d_%d" % (m, vp), [P, 2, 2048], U8) for vp in range(3)] for m in range(2)]
        w2s = [sb("w2s%d" % m, [P, 2, V], U8) for m in range(2)]
        he = [sb("he_%d" % i, [P, 2, 2, P, 2], BF16) for i in range(4)]
        hb0 = [sb("hb0_%d" % i, [P, 2, P, 4], BF16) for i in range(4)]
        hq0 = [sb("hq0_%d" % i, [P, 2, P], U32) for i in range(4)]
        hqs0 = [sb("hqs0_%d" % i, [P, 2, P], U8) for i in range(4)]
        hr1 = [sb("hr1_%d" % g, [P, 4, T], BF16) for g in range(2)]
        hb1 = [sb("hb1_%d" % g, [P, T, 4], BF16) for g in range(2)]
        hq1 = [sb("hq1_%d" % g, [P, T], U32) for g in range(2)]
        hqs1 = [sb("hqs1_%d" % g, [P, T], U8) for g in range(2)]
        ident = sb("ident", [P, P], F32)
        abf = sb("abf", [P, P], BF16)
        af = sb("af", [P, P], F32)
        nega = sb("nega", [P, 4], F32)
        warm = sb("warm", [P, 2], F32)

        def load_w1(m, lo, hi):
            nc.sync.dma_start(
                out=w1r[m][:, :, lo:hi].bitcast(I32),
                in_=w1_words[2 * m : 2 * m + 2, :, lo:hi].rearrange("g p c -> p g c").bitcast(I32),
            )

        def load_scales(tile, dram, m):
            src = dram[2 * m : 2 * m + 2].rearrange("g (q r) n -> r q g n", r=4)
            for r in range(4):
                nc.sync.dma_start(out=tile[r:P:32, :, :].bitcast(I32), in_=src[r].bitcast(I32))

        def load_w2(m, vp):
            nc.sync.dma_start(
                out=w2t[m][vp][:].bitcast(I32),
                in_=w2_words[2 * m : 2 * m + 2, :, 2048 * vp : 2048 * (vp + 1)].rearrange("g p c -> p g c").bitcast(I32),
            )

        def load_pair(tile, m, h):
            nc.sync.dma_start(out=tile[:], in_=x[m, 256 * h : 256 * (h + 1), :].rearrange("(i p) k -> p i k", i=2))

        def move(eng, out, in_):
            if eng == "s":
                nc.scalar.copy(out=out, in_=in_)
            else:
                nc.vector.tensor_copy(out=out, in_=in_)

        def relu(eng, out, in_):
            if eng == "s":
                nc.scalar.activation(out=out, in_=in_, func=RELU)
            else:
                nc.vector.tensor_scalar_max(out=out, in0=in_, scalar1=0.0)

        def turn(srcs):
            b = bank()
            bv = b[:].rearrange("p (g u r) -> p g u r", g=2, u=2)
            for g in range(2):
                for u in range(2):
                    nc.tensor.transpose(bv[:, g, u, :], srcs(g, u), ident[:])
            return bv.rearrange("p g u r -> p g r u")

        def words(t):
            return t.rearrange("p g r f -> p (g r f)").bitcast(F32).rearrange("p (g r u) -> p g r u", g=2, u=2)

        def deint(dst, x_tile):
            nc.vector.tensor_copy(out=dst[:], in_=x_tile.bitcast(F32).rearrange("p (g q u) -> p g u q", g=2, u=2))

        def tx0(i, eng):
            if i < 2:
                wd = x0a[i][:].bitcast(F32)
                bv = turn(lambda g, u: wd[:, 256 * g + u : 256 * (g + 1) : 2])
            else:
                bv = turn(lambda g, u: xe0[i - 2][:, g, u, :])
            move(eng, words(xg0[i][:]), bv)

        def tx1(i, eng):
            bv = turn(lambda g, u: xe1[i][:, g, u, :])
            move(eng, words(xg1[:])[:, :, P * i : P * (i + 1), :], bv)

        def th(i, eng):
            bv = turn(lambda g, u: he[i][:, g, u, :, :].rearrange("r p e -> r (p e)").bitcast(F32))
            move(eng, words(hb0[i][:]), bv)

        def quant(codes, scales, src):
            nc.vector.quantize_mx(out=codes.bitcast(FP8X4), scales=scales, in_=src)

        def qx0(i):
            quant(
                xq0[i][:].rearrange("p g r -> p (g r)"),
                xqs0[i][:].rearrange("p g r -> p (g r)"),
                xg0[i][:].rearrange("p g r f -> p (g r f)"),
            )

        def qh0(i):
            quant(
                hq0[i][:].rearrange("p g r -> p (g r)"),
                hqs0[i][:].rearrange("p g r -> p (g r)"),
                hb0[i][:].rearrange("p g r f -> p (g r f)"),
            )

        def qx1(g):
            quant(xq1[g][:], xqs1[g][:], xg1[:, g, :, :].rearrange("p r f -> p (r f)"))

        def qh1(g):
            quant(hq1[g][:], hqs1[g][:], hb1[g][:].rearrange("p r f -> p (r f)"))

        def perm_codes(G, t):
            nc.vector.tensor_copy(
                out=w1p[:, G, :, t, :].rearrange("p g (m e) -> p g m e", e=2),
                in_=w1r[1][:, :, 1024 * G : 1024 * (G + 1)].rearrange("p g (m t e) -> p g t m e", t=4, e=2)[:, :, t, :, :],
            )

        def perm_scales(G):
            nc.vector.tensor_copy(
                out=w1sp[:, G, :, :].rearrange("p g (t m) -> p g t m", t=4),
                in_=w1sr[1][:, :, 512 * G : 512 * (G + 1)].rearrange("p g (m t) -> p g t m", t=4),
            )

        def mm(b, lhsT, lhsT_scale, rhs, rhs_scale, g):
            nc.tensor.matmul_mx(
                out=b, lhsT=lhsT, lhsT_scale=lhsT_scale, rhs=rhs, rhs_scale=rhs_scale, start=(g == 0), stop=(g == 1)
            )

        def s1h(i, G, eng):
            b = bank()
            for g in range(2):
                mm(
                    b[:],
                    xq0[i][:, g, :].bitcast(FP8X4),
                    xqs0[i][:, g, :],
                    w1r[0][:, g, 1024 * G : 1024 * (G + 1)].bitcast(FP4X4),
                    w1sr[0][:, g, 512 * G : 512 * (G + 1)],
                    g,
                )
            relu(eng, he[i][:, G, :, :, :], b[:].rearrange("r (p u e) -> r u p e", u=2, e=2))

        def s1b(G, t, eng):
            b = bank()
            for g in range(2):
                mm(
                    b[:],
                    w1p[:, G, g, t, :].bitcast(FP4X4),
                    w1sp[:, G, g, P * t : P * (t + 1)],
                    xq1[g][:].bitcast(FP8X4),
                    xqs1[g][:],
                    g,
                )
            relu(eng, hr1[G][:, t, :], b[:])

        def il(G):
            nc.vector.tensor_copy(out=hb1[G][:], in_=hr1[G][:].rearrange("p t r -> p r t"))

        zs = {}

        def z0(v, i):
            b = bank()
            lo = 1024 * (v % 2)
            for G in range(2):
                mm(
                    b[:],
                    hq0[i][:, G, :].bitcast(FP8X4),
                    hqs0[i][:, G, :],
                    w2t[0][v // 2][:, G, lo : lo + 1024].bitcast(FP4X4),
                    w2s[0][:, G, 512 * v : 512 * (v + 1)],
                    G,
                )
            z = zpool.tile([P, 512], F32, name="z")
            nc.scalar.copy(out=z[:], in_=b[:])
            zs[(v, i)] = z

        def z1(v, i, parts):
            o = opool.tile([P, 512], F32, name="o")
            toks = slice(P * i, P * (i + 1))
            for part in range(parts):
                b = bank()
                w = 512 // parts
                n = 512 if parts == 1 else P
                for c in range(0, w, n):
                    col = part * w + c
                    lo = 1024 * (v % 2) + 2 * col
                    for G in range(2):
                        mm(
                            b[:, c : c + n],
                            hq1[G][:, toks].bitcast(FP8X4),
                            hqs1[G][:, toks],
                            w2t[1][v // 2][:, G, lo : lo + 2 * n].bitcast(FP4X4),
                            w2s[1][:, G, 512 * v + col : 512 * v + col + n],
                            G,
                        )
                cols = slice(part * w, (part + 1) * w)
                nc.vector.scalar_tensor_tensor(
                    out=o[:, cols], in0=b[:, 0:w], scalar=nega[:, i : i + 1], in1=zs[(v, i)][:, cols], op0=MULT, op1=ADD
                )
                nc.sync.dma_start(out=out[toks, 512 * v + part * w : 512 * v + (part + 1) * w], in_=o[:, cols])

        nc.sync.dma_start(out=x0a[0][:], in_=x[0, 0:P, :])
        load_w1(0, 0, 1024)
        nc.gpsimd.memset(warm[:], 0.0)
        nc.scalar.dma_start(out=abf[0:4, :], in_=alpha.rearrange("(i p) -> i p", p=P))
        nc.scalar.activation(out=warm[:, 0:1], in_=warm[:, 1:2], func=RELU)
        for t in (w1sr[0], w1sr[1], w2s[0], w2s[1]):
            nc.vector.memset(t[:].bitcast(I32), 0)
        make_identity(nc, ident[:])
        nc.gpsimd.memset(af[:], 0.0)
        load_scales(w1sr[0], w1_scales, 0)
        nc.sync.dma_start(out=x0a[1][:], in_=x[0, P : 2 * P, :])
        load_w1(0, 1024, 2048)
        load_pair(x0b, 0, 1)
        load_scales(w1sr[1], w1_scales, 1)
        load_w1(1, 0, 2048)
        load_pair(x1[0], 1, 0)
        load_pair(x1[1], 1, 1)
        load_scales(w2s[0], w2_scales, 0)
        load_w2(0, 0)
        load_w2(0, 1)
        load_w2(0, 2)
        load_scales(w2s[1], w2_scales, 1)
        for vp in range(3):
            load_w2(1, vp)

        tx0(0, "s")
        qx0(0)
        tx0(1, "s")
        s1h(0, 0, "s")
        qx0(1)
        s1h(0, 1, "s")
        for i in range(2):
            deint(xe0[i], x0b[:, i, :])
        tx0(2, "s")
        tx0(3, "v")
        qx0(2)
        qx0(3)
        for t in range(3):
            perm_codes(0, t)
        for i in (1, 2, 3):
            s1h(i, 0, "s")
            s1h(i, 1, "s" if i == 1 else "v")
            if i == 2:
                perm_codes(0, 3)
                for j in range(2):
                    deint(xe1[j], x1[0][:, j, :])
        for j in range(2):
            deint(xe1[2 + j], x1[1][:, j, :])
        th(0, "s")
        th(1, "s")
        th(2, "v")
        qh0(0)
        tx1(0, "s")
        qh0(1)
        tx1(1, "s")
        qh0(2)
        th(3, "s")
        tx1(2, "v")
        qh0(3)
        tx1(3, "s")
        nc.scalar.activation(out=af[0:4, :], in_=abf[0:4, :], func=COPY, scale=-1.0)
        ba = bank()
        nc.tensor.transpose(ba[:, 0:P], af[:], ident[:])
        nc.vector.tensor_copy(out=nega[:], in_=ba[:, 0:4])
        perm_scales(0)
        qx1(0)
        qx1(1)
        perm_scales(1)
        for t in range(4):
            perm_codes(1, t)

        order = [(v, i) for v in range(2) for i in range(3)] + [(0, 3), (1, 3)]
        order += [(v, i) for v in range(2, 6) for i in range(4)]
        for k in range(8):
            z0(*order[k])
        for G in range(2):
            for t in range(4):
                s1b(G, t, "v" if (G == 0 and t % 2 == 1) else "s")
            il(G)
            qh1(G)
            if G == 0:
                z0(*order[8])
        for k in range(9, 16):
            z0(*order[k])
        done0 = 16
        for k in range(24):
            z1(*order[k], 2 if k == 23 else 1)
            if done0 < 24 and done0 - (k + 1) <= 3:
                z0(*order[done0])
                done0 += 1
